import numpy as np
import ml_dtypes


def mxq(x, axis, fmt="e4m3"):
    dtype, down = {"e4m3": (ml_dtypes.float8_e4m3fn, 7), "e5m2": (ml_dtypes.float8_e5m2, 14)}[fmt]
    v = np.moveaxis(np.asarray(x, np.float32).astype(ml_dtypes.bfloat16).astype(np.float64), axis, -1)
    blocks = v.reshape(v.shape[:-1] + (-1, 32))
    amax = np.abs(blocks).max(-1, keepdims=True)
    byte = np.maximum(np.where(amax > 0, np.frexp(amax)[1] - 1 + 127, 0) - down, 1)
    scale = np.exp2(byte - 127.0)
    codes = (blocks / scale).astype(np.float32).astype(dtype).astype(np.float64)
    return np.moveaxis((codes * scale).reshape(v.shape), -1, axis)


WIDE = False


def mx_kscale(k):
    if not WIDE:
        return np.ones(k)
    levels = np.array([10, -10, 5, -5, 0])
    if k % 512:
        return np.exp2(np.random.permutation(np.resize(levels, k // 32))).repeat(32)
    a = np.empty((k // 512, 16))
    for p in range(k // 512):
        a[p, :8] = np.random.permutation(np.resize(levels, 8))
        for g in range(8):
            far = levels[np.abs(levels - a[p, g]) >= 10]
            a[p, g + 8] = far[np.random.randint(len(far))]
    return np.exp2(a.ravel()).repeat(32)


def f64(x):
    return np.asarray(x).astype(np.float64)


def striped(idx):
    return np.tile(idx.reshape(-1, 16).T, (8, 1)).astype(np.uint16)


def unstriped(offs):
    return offs[:16].T.reshape(-1).astype(np.int64)


def striped8(idx):
    return np.concatenate([x.reshape(-1, 16).T for x in idx]).astype(np.uint16)


def runs(offs, k):
    lists = np.stack([offs[16 * r : 16 * r + 16].T.reshape(-1) for r in range(8)]).astype(np.int64)
    return lists[np.arange(k) % 512 // 64]


def pack_weight(w):
    k, n = w.shape
    w = f64(np.asarray(w, np.float32).astype(ml_dtypes.bfloat16)).reshape(k // 32, 32, n)
    amax = np.abs(w).max(1)
    byte = np.clip(np.where(amax > 0, np.frexp(amax)[1] - 1 + 127 - 7, 1), 1, 254)
    scaled = (w * np.exp2(127.0 - byte)[:, None, :]).reshape(k, n).astype(np.float32)
    words = np.ascontiguousarray(scaled.reshape(k // 512, 128, 4, n).transpose(0, 1, 3, 2)).astype(ml_dtypes.float8_e4m3fn).view(np.uint8)
    return words, np.ascontiguousarray(byte.astype(np.uint8).reshape(k // 512, 16, n))


def unpack_weight(words, scales):
    g, p, n, _ = words.shape
    vals = np.ascontiguousarray(words).view(ml_dtypes.float8_e4m3fn).astype(np.float64) * np.repeat(np.exp2(scales.astype(np.float64) - 127.0), 8, axis=1)[..., None]
    return vals.transpose(0, 1, 3, 2).reshape(g * 512, n)


K, T, S, N, H, G, W = 512, 1024, 512, 512, 512, 2048, 384


def setup_inputs():
    n = np.random.standard_normal
    s = mx_kscale(K)[:, None]
    u = mx_kscale(S)
    packed_xT = pack_weight(n((K, T)) * s)
    packed_dT = pack_weight(n((K, G)) / s)
    return {
        "x_words": packed_xT[0],
        "x_scales": packed_xT[1],
        "w1": (n((K, H)) / np.sqrt(K) / s).astype(np.float32),
        "d_words": packed_dT[0],
        "d_scales": packed_dT[1],
        "gn": (np.random.uniform(0.5, 1.5, (H, 1)) * u[:, None]).astype(np.float32),
        "gk": (np.random.uniform(0.5, 1.5, (H, 1)) * u[:, None]).astype(np.float32),
        "w2": (n((H, N)) / np.sqrt(2 * H) / u[:, None]).astype(np.float32),
        "w3": (n((H, N)) / np.sqrt(2 * H) / u[:, None]).astype(np.float32),
        "offs": striped(np.random.permutation(T)[:S]),
        "kidx": striped8(np.random.randint(0, G, (8, H))),
        "two": striped(np.random.permutation(T)[:S]),
        "n1": striped(np.random.permutation(S)[:W]),
        "n2": striped(np.random.permutation(S)[:W]),
        "n3": striped(np.random.permutation(S)[:W]),
        "n4": striped(np.random.permutation(S)[:W]),
        "n5": striped8(np.stack([np.random.permutation(S) for _ in range(8)])),
        "n6": striped8(np.stack([np.random.permutation(S) for _ in range(8)])),
    }


def reference(x_words, x_scales, w1, d_words, d_scales, gn, gk, w2, w3, offs, kidx, two, n1, n2, n3, n4, n5, n6):
    xq = unpack_weight(x_words, x_scales)[:, unstriped(offs)]
    y = mxq(f64(w1), 0, "e4m3").T @ xq
    old = y[:, unstriped(n1)]
    pa = y[:, unstriped(n2)]
    ra = old - (0.5 * pa)
    ds = y.copy()
    ds[:, unstriped(n1)] = ra
    z = f64(gn) * ds
    d_kidx = unpack_weight(d_words, d_scales)[np.arange(K)[:, None], runs(kidx, K)]
    x_two = unpack_weight(x_words, x_scales)[:, unstriped(two)]
    s = 0.0625 * (d_kidx.T @ x_two)
    old2 = s[:, unstriped(n3)]
    pa2 = s[:, unstriped(n4)]
    ra2 = old2 / (np.abs(pa2) + 0.5)
    ds2 = s.copy()
    ds2[:, unstriped(n3)] = ra2
    z2 = f64(gk) * ds2
    h = mxq(f64(w2), 0, "e4m3").T @ mxq(z, 0, "e4m3") + mxq(f64(w3), 0, "e4m3").T @ mxq(z2, 0, "e4m3")
    return (np.tanh(h[np.arange(N)[:, None], runs(n5, N)] - h)) * (h[np.arange(N)[:, None], runs(n6, N)])

@@ -1,0 +1,265 @@
+from contextlib import ExitStack
+
+import concourse.mybir as mybir
+
+K, T, S, N, H, G, W = 512, 1024, 512, 512, 512, 2048, 384
+FLOPS = 4 * 2 * 512 * 512 * 512
+
+F32 = mybir.dt.float32
+BF16 = mybir.dt.bfloat16
+I32 = mybir.dt.int32
+U32 = mybir.dt.uint32
+U16 = mybir.dt.uint16
+U8 = mybir.dt.uint8
+FP8X4 = mybir.dt.float8_e4m3fn_x4
+ALU = mybir.AluOpType
+ACT = mybir.ActivationFunctionType
+
+P = 128
+PACK = 4
+HALF = 256
+
+
+def tile_picked_jkeykdifknormfdif_none_p_kernel(
+    tc, x_words, x_scales, w1, d_words, d_scales, gn, gk, w2, w3, offs, kidx, two, n1, n2, n3, n4, n5, n6, out
+):
+    nc = tc.nc
+    with ExitStack() as ctx:
+        keep = ctx.enter_context(tc.tile_pool(name="keep", bufs=1))
+        psum = ctx.enter_context(tc.psum_pool(name="psum", bufs=1))
+
+        def sb(name, shape, dtype):
+            return keep.tile(shape, dtype, name=name, align_bytes=64)
+
+        def load_list(name, src):
+            t = keep.tile([P, src.shape[1]], U16, name=name)
+            nc.sync.dma_start(t[:], src)
+            return t
+
+        def load_weight(name, w, lo, hi, tag):
+            raw = keep.tile([P, PACK, hi - lo], F32, name=name, tag=tag, align_bytes=64)
+            nc.sync.dma_start(raw[:], w.rearrange("(p j) c -> p j c", j=PACK)[:, :, lo:hi])
+            return raw
+
+        xs_tab = sb("xs_tab", [P, T], U8)
+        ds_tab = sb("ds_tab", [P, G], U8)
+        ds_fin = sb("ds_fin", [P, H], U8)
+        half = sb("half", [P, 1], F32)
+        nc.gpsimd.memset(xs_tab[:].bitcast(I32), 0)
+        nc.gpsimd.memset(ds_tab[:].bitcast(I32), 0)
+        nc.gpsimd.memset(ds_fin[:].bitcast(I32), 0)
+        nc.gpsimd.memset(half[:], 0.5)
+
+        l_offs = load_list("l_offs", offs)
+        xw_tab = sb("xw_tab", [P, T], I32)
+        nc.sync.dma_start(xw_tab[:], x_words[0].rearrange("p n t -> p (n t)").bitcast(I32))
+        for q in range(4):
+            nc.scalar.dma_start(xs_tab[32 * q : 32 * q + 4, :].bitcast(I32), x_scales[0, 4 * q : 4 * q + 4, :].bitcast(I32))
+        w1_raw = [load_weight("w1_raw%d" % u, w1, u * HALF, (u + 1) * HALF, "raw%d" % u) for u in range(2)]
+        l_kidx = load_list("l_kidx", kidx)
+        nc.scalar.dma_start(ds_tab[0:P:8, :].bitcast(I32), d_scales[0].bitcast(I32))
+        gn_sb = sb("gn_sb", [P, PACK], F32)
+        gk_sb = sb("gk_sb", [P, PACK], F32)
+        nc.sync.dma_start(gn_sb[:], gn.rearrange("(p t) o -> p (t o)", t=PACK))
+        l_n2 = load_list("l_n2", n2)
+        l_n1 = load_list("l_n1", n1)
+        dw_tab = sb("dw_tab", [P, G], I32)
+        nc.sync.dma_start(dw_tab[:], d_words[0].rearrange("p n t -> p (n t)").bitcast(I32))
+        l_two = load_list("l_two", two)
+        nc.sync.dma_start(gk_sb[:], gk.rearrange("(p t) o -> p (t o)", t=PACK))
+        l_n4 = load_list("l_n4", n4)
+        l_n3 = load_list("l_n3", n3)
+
+        def gather_packed(name, tab, lst, dtype):
+            g = sb(name, [P, S], dtype)
+            src = tab[:].bitcast(U32) if dtype == U32 else tab[:]
+            nc.vector.tensor_copy(g[:], src.indirect(lst[:]))
+            return g
+
+        def quantize(codes, scales, grouped, lo, hi):
+            nc.vector.quantize_mx(out=codes[:, lo:hi].bitcast(FP8X4), scales=scales[:, lo:hi], in_=grouped[:, PACK * lo : PACK * hi])
+
+        def deal_views(grouped, raw, m0):
+            width = raw.shape[2] // PACK
+            dst = grouped[:].rearrange("p (t m j) -> p m j t", t=PACK, j=PACK)[:, m0 : m0 + width, :, :]
+            src = raw[:].rearrange("p j (m t) -> p m j t", t=PACK)
+            return dst, src
+
+        def mx(bank, lhs, lhs_s, t, rhs, rhs_s, start, stop):
+            cols = slice(t * P, (t + 1) * P)
+            nc.tensor.matmul_mx(out=bank[:], lhsT=lhs[:, cols].bitcast(FP8X4), lhsT_scale=lhs_s[:, cols],
+                                rhs=rhs[:].bitcast(FP8X4), rhs_scale=rhs_s[:], start=start, stop=stop)
+
+        x1w = gather_packed("x1w", xw_tab, l_offs, U32)
+        x1s = gather_packed("x1s", xs_tab, l_offs, U8)
+        w1_g = sb("w1_g", [P, PACK * H], BF16)
+        for u in range(2):
+            dst, src = deal_views(w1_g, w1_raw[u], u * HALF // PACK)
+            nc.scalar.copy(dst, src)
+        dsg = gather_packed("dsg", ds_tab, l_kidx, U8)
+        ds_deal = sb("ds_deal", [P, H], U8)
+        nc.vector.tensor_copy(ds_deal[:].rearrange("p (t m) -> p m t", t=PACK), dsg[:].rearrange("p (m t) -> p m t", t=PACK))
+        for u in range(4):
+            nc.scalar.dma_start(ds_fin[u:P:32, :].bitcast(I32), ds_deal[8 * u : P : 32, :].bitcast(I32))
+        w3_raw = load_weight("w3_raw", w3, 0, N, "raw0")
+        l_n5 = load_list("l_n5", n5)
+        l_n6 = load_list("l_n6", n6)
+        w1_c = sb("w1_c", [P, H], U32)
+        w1_s = sb("w1_s", [P, H], U8)
+        y_bank = [psum.tile([P, S], F32, name="bankA%d" % t) for t in range(PACK)]
+        for t in range(PACK):
+            quantize(w1_c, w1_s, w1_g, t * P, (t + 1) * P)
+            mx(y_bank[t], w1_c, w1_s, t, x1w, x1s, True, True)
+
+        x2w = gather_packed("x2w", xw_tab, l_two, U32)
+        x2s = gather_packed("x2s", xs_tab, l_two, U8)
+        dwg = gather_packed("dwg", dw_tab, l_kidx, U32)
+        dw_deal = sb("dw_deal", [P, H], U32)
+        nc.vector.tensor_copy(dw_deal[:].rearrange("p (t m) -> p t m", t=PACK), dwg[:].rearrange("p (m t) -> p t m", t=PACK))
+        s_bank = [psum.tile([P, S], F32, name="bankB%d" % t) for t in range(PACK)]
+        for t in range(PACK):
+            mx(s_bank[t], dw_deal, ds_fin, t, x2w, x2s, True, True)
+        gk16 = sb("gk16", [P, PACK], F32)
+        nc.gpsimd.tensor_scalar(gk16[:], gk_sb[:], 0.0625, 0.0, ALU.mult, ALU.add)
+
+        z_all = sb("z_all", [P, PACK - 2, S], F32)
+        z2_all = sb("z2_all", [P, PACK - 1, S], F32)
+        yt, st, pa, ra, rs, rb = {}, {}, {}, {}, {}, {}
+
+        def y_fetch(t):
+            yt[t] = sb("y%d" % t, [P, S], F32)
+            nc.scalar.activation(yt[t][:], y_bank[t][:], ACT.Copy, scale=gn_sb[:, t : t + 1])
+            pa[t] = sb("pa%d" % t, [P, W], F32)
+            nc.scalar.activation(pa[t][:], yt[t][:].indirect(l_n2[:]), ACT.Copy, scale=-0.5)
+
+        def y_mix(t):
+            ra[t] = sb("ra%d" % t, [P, W], F32)
+            nc.vector.tensor_tensor(ra[t][:], yt[t][:].indirect(l_n1[:]), pa[t][:], ALU.add)
+
+        def y_put(t):
+            nc.scalar.activation(yt[t][:].indirect(l_n1[:]), ra[t][:], ACT.Copy)
+            if t < PACK - 2:
+                nc.sync.dma_start(z_all[:, t, :], yt[t][:])
+
+        def s_fetch(t):
+            mag = keep.tile([P, S], F32, name="mag%d" % t, tag="raw1" if t == 0 else "mag%d" % t, align_bytes=64)
+            nc.scalar.activation(mag[:], s_bank[t][:], ACT.Abs, scale=0.0625)
+            den = sb("den%d" % t, [P, W], F32)
+            nc.scalar.activation(den[:], mag[:].indirect(l_n4[:]), ACT.Copy)
+            st[t] = sb("s%d" % t, [P, S], F32)
+            nc.scalar.activation(st[t][:], s_bank[t][:], ACT.Copy, scale=gk16[:, t : t + 1])
+            rs[t] = sb("rs%d" % t, [P, W], F32)
+            nc.scalar.activation(rs[t][:], den[:], ACT.Abs_reciprocal_sqrt, bias=half[:])
+
+        def s_mix(t):
+            rb[t] = sb("rb%d" % t, [P, W], F32)
+            nc.vector.tensor_tensor(rb[t][:], st[t][:].indirect(l_n3[:]), rs[t][:], ALU.mult)
+
+        def s_put(t):
+            nc.vector.tensor_tensor(st[t][:].indirect(l_n3[:]), rb[t][:], rs[t][:], ALU.mult)
+            if t < PACK - 1:
+                nc.sync.dma_start(z2_all[:, t, :], st[t][:])
+
+        w_g = {}
+        w_c = {}
+        w_s = {}
+
+        def w_deal(name, raw, copy):
+            w_g[name] = sb(name + "_g", [P, PACK * N], BF16)
+            dst, src = deal_views(w_g[name], raw, 0)
+            copy(dst, src)
+
+        def w_quant(name):
+            w_c[name] = sb(name + "_c", [P, N], U32)
+            w_s[name] = sb(name + "_s", [P, N], U8)
+            quantize(w_c[name], w_s[name], w_g[name], 0, N)
+
+        z_g, z_c, z_s = {}, {}, {}
+
+        def weave_first(name, planes):
+            z_g[name] = sb(name + "_g", [P, PACK * S], BF16)
+            view = z_g[name][:].rearrange("p (c i t) -> p c t i", i=4, t=PACK)
+            nc.vector.tensor_copy(view[:, :, 0 : planes.shape[1], :], planes[:].rearrange("p t (c i) -> p c t i", i=4))
+
+        def weave_one(name, t, plane):
+            nc.vector.tensor_copy(z_g[name][:].rearrange("p (c t) -> p c t", t=PACK)[:, :, t], plane[:])
+
+        def z_quant(name):
+            z_c[name] = sb(name + "_c", [P, S], U32)
+            z_s[name] = sb(name + "_s", [P, S], U8)
+            quantize(z_c[name], z_s[name], z_g[name], 0, S)
+
+        for t in range(PACK):
+            y_fetch(t)
+            y_mix(t)
+        s_fetch(0)
+        w2_raw = load_weight("w2_raw", w2, 0, N, "raw1")
+        w_deal("w3", w3_raw, nc.vector.tensor_copy)
+        w_quant("w3")
+        for t in range(PACK - 1):
+            s_mix(t)
+            s_fetch(t + 1)
+            s_put(t)
+        y_put(0)
+        s_mix(3)
+        y_put(1)
+        s_put(3)
+        weave_first("z2", z2_all)
+        weave_one("z2", 3, st[3])
+        y_put(2)
+        weave_first("z", z_all)
+        z_quant("z2")
+        h_bank = [psum.tile([P, S], F32, name="bankA%d" % t) for t in range(PACK)]
+        for t in range(PACK):
+            mx(h_bank[t], w_c["w3"], w_s["w3"], t, z_c["z2"], z_s["z2"], True, False)
+        y_put(3)
+        w_deal("w2", w2_raw, nc.scalar.copy)
+        weave_one("z", 2, yt[2])
+        weave_one("z", 3, yt[3])
+        w_quant("w2")
+        z_quant("z")
+        for t in range(PACK):
+            mx(h_bank[t], w_c["w2"], w_s["w2"], t, z_c["z"], z_s["z"], False, True)
+
+        out_v = out.rearrange("(p t) n -> p t n", t=PACK)
+        ht, pick, df, th = {}, {}, {}, {}
+
+        def h_window(t, copy):
+            ht[t] = sb("h%d" % t, [P, 2 * S], F32)
+            copy(ht[t][:, 0:S], h_bank[t][:])
+
+        def h_pick(t):
+            pick[t] = sb("pick%d" % t, [P, S], F32)
+            nc.scalar.activation(pick[t][:], ht[t][:].indirect(l_n5[:]), ACT.Copy)
+
+        def h_diff(t):
+            df[t] = sb("df%d" % t, [P, S], F32)
+            nc.vector.tensor_tensor(df[t][:], pick[t][:], h_bank[t][:], ALU.subtract)
+
+        def h_tanh(t):
+            th[t] = sb("th%d" % t, [P, S], F32)
+            nc.scalar.activation(th[t][:], df[t][:], ACT.Tanh)
+
+        def h_out(t, pieces):
+            width = S // pieces
+            for u in range(pieces):
+                res = sb("res%d_%d" % (t, u), [P, width], F32)
+                cols = slice(u * width, (u + 1) * width)
+                offsets = l_n6[:, u * width // 16 : (u + 1) * width // 16]
+                nc.vector.tensor_tensor(res[:], ht[t][:].indirect(offsets), th[t][:, cols], ALU.mult)
+                nc.sync.dma_start(out_v[:, t, cols], res[:])
+
+        h_window(0, nc.scalar.copy)
+        h_pick(0)
+        for t in range(1, PACK):
+            h_window(t, nc.vector.tensor_copy)
+        h_pick(1)
+        h_diff(0)
+        h_tanh(0)
+        for t in range(1, PACK):
+            h_diff(t)
+            if t + 1 < PACK:
+                h_pick(t + 1)
+            h_out(t - 1, 1)
+            h_tanh(t)
+        h_out(PACK - 1, 2)

@@ -47,31 +47,34 @@ def tile_picked_jkeykdifknormfdif_none_p_kernel(
         half = sb("half", [P, 1], F32)
         nc.gpsimd.memset(xs_tab[:].bitcast(I32), 0)
         nc.gpsimd.memset(ds_tab[:].bitcast(I32), 0)
-        nc.gpsimd.memset(ds_fin[:].bitcast(I32), 0)
         nc.gpsimd.memset(half[:], 0.5)
+        nc.gpsimd.memset(ds_fin[:].bitcast(I32), 0)
 
         l_offs = load_list("l_offs", offs)
+        l_kidx = load_list("l_kidx", kidx)
         xw_tab = sb("xw_tab", [P, T], I32)
         nc.sync.dma_start(xw_tab[:], x_words[0].rearrange("p n t -> p (n t)").bitcast(I32))
+        l_two = load_list("l_two", two)
         for q in range(4):
-            nc.scalar.dma_start(xs_tab[32 * q : 32 * q + 4, :].bitcast(I32), x_scales[0, 4 * q : 4 * q + 4, :].bitcast(I32))
-        w1_raw = [load_weight("w1_raw%d" % u, w1, u * HALF, (u + 1) * HALF, "raw%d" % u) for u in range(2)]
-        l_kidx = load_list("l_kidx", kidx)
+            nc.sync.dma_start(xs_tab[32 * q : 32 * q + 4, :].bitcast(I32), x_scales[0, 4 * q : 4 * q + 4, :].bitcast(I32))
         nc.scalar.dma_start(ds_tab[0:P:8, :].bitcast(I32), d_scales[0].bitcast(I32))
-        gn_sb = sb("gn_sb", [P, PACK], F32)
-        gk_sb = sb("gk_sb", [P, PACK], F32)
-        nc.sync.dma_start(gn_sb[:], gn.rearrange("(p t) o -> p (t o)", t=PACK))
+        warm = sb("warm", [P, 2], F32)
+        nc.scalar.activation(warm[:, 0:1], half[:], ACT.Abs_reciprocal_sqrt, bias=half[:])
+        w1_raw = [load_weight("w1_raw%d" % u, w1, u * HALF, (u + 1) * HALF, "raw%d" % u) for u in range(2)]
+        w3_lo = load_weight("w3_lo", w3, 0, HALF, "w3_lo")
         l_n2 = load_list("l_n2", n2)
         l_n1 = load_list("l_n1", n1)
         dw_tab = sb("dw_tab", [P, G], I32)
         nc.sync.dma_start(dw_tab[:], d_words[0].rearrange("p n t -> p (n t)").bitcast(I32))
-        l_two = load_list("l_two", two)
-        nc.sync.dma_start(gk_sb[:], gk.rearrange("(p t) o -> p (t o)", t=PACK))
+        gn_sb = sb("gn_sb", [P, PACK], F32)
+        gk_sb = sb("gk_sb", [P, PACK], F32)
+        nc.gpsimd.dma_start(gn_sb[:], gn.rearrange("(p t) o -> p (t o)", t=PACK))
+        nc.gpsimd.dma_start(gk_sb[:], gk.rearrange("(p t) o -> p (t o)", t=PACK))
         l_n4 = load_list("l_n4", n4)
         l_n3 = load_list("l_n3", n3)
 
-        def gather_packed(name, tab, lst, dtype):
-            g = sb(name, [P, S], dtype)
+        def gather_packed(name, tab, lst, dtype, tag=None):
+            g = keep.tile([P, S], dtype, name=name, tag=tag or name, align_bytes=64)
             src = tab[:].bitcast(U32) if dtype == U32 else tab[:]
             nc.vector.tensor_copy(g[:], src.indirect(lst[:]))
             return g
@@ -85,10 +88,10 @@ def tile_picked_jkeykdifknormfdif_none_p_kernel(
             src = raw[:].rearrange("p j (m t) -> p m j t", t=PACK)
             return dst, src
 
-        def mx(bank, lhs, lhs_s, t, rhs, rhs_s, start, stop):
+        def mx(bank, lhs, lhs_s, t, rhs, rhs_s, start, stop, lo=0, hi=S):
             cols = slice(t * P, (t + 1) * P)
-            nc.tensor.matmul_mx(out=bank[:], lhsT=lhs[:, cols].bitcast(FP8X4), lhsT_scale=lhs_s[:, cols],
-                                rhs=rhs[:].bitcast(FP8X4), rhs_scale=rhs_s[:], start=start, stop=stop)
+            nc.tensor.matmul_mx(out=bank[:, lo:hi], lhsT=lhs[:, cols].bitcast(FP8X4), lhsT_scale=lhs_s[:, cols],
+                                rhs=rhs[:, lo:hi].bitcast(FP8X4), rhs_scale=rhs_s[:, lo:hi], start=start, stop=stop)
 
         x1w = gather_packed("x1w", xw_tab, l_offs, U32)
         x1s = gather_packed("x1s", xs_tab, l_offs, U8)
@@ -96,12 +99,6 @@ def tile_picked_jkeykdifknormfdif_none_p_kernel(
         for u in range(2):
             dst, src = deal_views(w1_g, w1_raw[u], u * HALF // PACK)
             nc.scalar.copy(dst, src)
-        dsg = gather_packed("dsg", ds_tab, l_kidx, U8)
-        ds_deal = sb("ds_deal", [P, H], U8)
-        nc.vector.tensor_copy(ds_deal[:].rearrange("p (t m) -> p m t", t=PACK), dsg[:].rearrange("p (m t) -> p m t", t=PACK))
-        for u in range(4):
-            nc.scalar.dma_start(ds_fin[u:P:32, :].bitcast(I32), ds_deal[8 * u : P : 32, :].bitcast(I32))
-        w3_raw = load_weight("w3_raw", w3, 0, N, "raw0")
         l_n5 = load_list("l_n5", n5)
         l_n6 = load_list("l_n6", n6)
         w1_c = sb("w1_c", [P, H], U32)
@@ -111,6 +108,12 @@ def tile_picked_jkeykdifknormfdif_none_p_kernel(
             quantize(w1_c, w1_s, w1_g, t * P, (t + 1) * P)
             mx(y_bank[t], w1_c, w1_s, t, x1w, x1s, True, True)
 
+        dsg = gather_packed("dsg", ds_tab, l_kidx, U8, "raw1")
+        ds_deal = sb("ds_deal", [P, H], U8)
+        nc.vector.tensor_copy(ds_deal[:].rearrange("p (t m) -> p m t", t=PACK), dsg[:].rearrange("p (m t) -> p m t", t=PACK))
+        for u in range(4):
+            nc.sync.dma_start(ds_fin[u:P:32, :].bitcast(I32), ds_deal[8 * u : P : 32, :].bitcast(I32))
+        w2_lo = load_weight("w2_lo", w2, 0, HALF, "raw1")
         x2w = gather_packed("x2w", xw_tab, l_two, U32)
         x2s = gather_packed("x2s", xs_tab, l_two, U8)
         dwg = gather_packed("dwg", dw_tab, l_kidx, U32)
@@ -122,34 +125,34 @@ def tile_picked_jkeykdifknormfdif_none_p_kernel(
         gk16 = sb("gk16", [P, PACK], F32)
         nc.gpsimd.tensor_scalar(gk16[:], gk_sb[:], 0.0625, 0.0, ALU.mult, ALU.add)
 
-        z_all = sb("z_all", [P, PACK - 2, S], F32)
+        z_all = sb("z_all", [P, PACK - 1, S], F32)
         z2_all = sb("z2_all", [P, PACK - 1, S], F32)
-        yt, st, pa, ra, rs, rb = {}, {}, {}, {}, {}, {}
+        ra = keep.tile([P, PACK, W], F32, name="ra", tag="dw_tab", align_bytes=64)
+        yt, st, pa, rs, rb = {}, {}, {}, {}, {}
 
         def y_fetch(t):
-            yt[t] = sb("y%d" % t, [P, S], F32)
-            nc.scalar.activation(yt[t][:], y_bank[t][:], ACT.Copy, scale=gn_sb[:, t : t + 1])
+            yt[t] = sb("y%d" % t, [P, S + W], F32)
+            nc.scalar.activation(yt[t][:, 0:S], y_bank[t][:], ACT.Copy, scale=gn_sb[:, t : t + 1])
             pa[t] = sb("pa%d" % t, [P, W], F32)
             nc.scalar.activation(pa[t][:], yt[t][:].indirect(l_n2[:]), ACT.Copy, scale=-0.5)
 
         def y_mix(t):
-            ra[t] = sb("ra%d" % t, [P, W], F32)
-            nc.vector.tensor_tensor(ra[t][:], yt[t][:].indirect(l_n1[:]), pa[t][:], ALU.add)
+            nc.vector.tensor_tensor(ra[:, t, :], yt[t][:].indirect(l_n1[:]), pa[t][:], ALU.add)
 
         def y_put(t):
-            nc.scalar.activation(yt[t][:].indirect(l_n1[:]), ra[t][:], ACT.Copy)
-            if t < PACK - 2:
-                nc.sync.dma_start(z_all[:, t, :], yt[t][:])
+            nc.scalar.activation(yt[t][:].indirect(l_n1[:]), ra[:, t, :], ACT.Copy)
+            if t < PACK - 1:
+                nc.sync.dma_start(z_all[:, t, :], yt[t][:, 0:S])
 
         def s_fetch(t):
-            mag = keep.tile([P, S], F32, name="mag%d" % t, tag="raw1" if t == 0 else "mag%d" % t, align_bytes=64)
+            mag = sb("mag%d" % t, [P, S], F32)
             nc.scalar.activation(mag[:], s_bank[t][:], ACT.Abs, scale=0.0625)
-            den = sb("den%d" % t, [P, W], F32)
-            nc.scalar.activation(den[:], mag[:].indirect(l_n4[:]), ACT.Copy)
+            den = yt[t][:, S : S + W]
+            nc.scalar.activation(den, mag[:].indirect(l_n4[:]), ACT.Copy)
             st[t] = sb("s%d" % t, [P, S], F32)
             nc.scalar.activation(st[t][:], s_bank[t][:], ACT.Copy, scale=gk16[:, t : t + 1])
             rs[t] = sb("rs%d" % t, [P, W], F32)
-            nc.scalar.activation(rs[t][:], den[:], ACT.Abs_reciprocal_sqrt, bias=half[:])
+            nc.scalar.activation(rs[t][:], den, ACT.Abs_reciprocal_sqrt, bias=half[:])
 
         def s_mix(t):
             rb[t] = sb("rb%d" % t, [P, W], F32)
@@ -164,9 +167,10 @@ def tile_picked_jkeykdifknormfdif_none_p_kernel(
         w_c = {}
         w_s = {}
 
-        def w_deal(name, raw, copy):
-            w_g[name] = sb(name + "_g", [P, PACK * N], BF16)
-            dst, src = deal_views(w_g[name], raw, 0)
+        def w_deal(name, raw, m0, copy):
+            if name not in w_g:
+                w_g[name] = sb(name + "_g", [P, PACK * N], BF16)
+            dst, src = deal_views(w_g[name], raw, m0)
             copy(dst, src)
 
         def w_quant(name):
@@ -176,50 +180,67 @@ def tile_picked_jkeykdifknormfdif_none_p_kernel(
 
         z_g, z_c, z_s = {}, {}, {}
 
-        def weave_first(name, planes):
-            z_g[name] = sb(name + "_g", [P, PACK * S], BF16)
+        def weave_first(name, planes, copy):
+            z_g[name] = keep.tile([P, PACK * S], BF16, name=name + "_g", tag="rs3", align_bytes=64)
             view = z_g[name][:].rearrange("p (c i t) -> p c t i", i=4, t=PACK)
-            nc.vector.tensor_copy(view[:, :, 0 : planes.shape[1], :], planes[:].rearrange("p t (c i) -> p c t i", i=4))
+            copy(view[:, :, 0 : planes.shape[1], :], planes[:].rearrange("p t (c i) -> p c t i", i=4))
 
-        def weave_one(name, t, plane):
-            nc.vector.tensor_copy(z_g[name][:].rearrange("p (c t) -> p c t", t=PACK)[:, :, t], plane[:])
+        def weave_one(name, t, plane, lo, hi):
+            nc.vector.tensor_copy(z_g[name][:].rearrange("p (c t) -> p c t", t=PACK)[:, lo:hi, t], plane[:, lo:hi])
 
-        def z_quant(name):
-            z_c[name] = sb(name + "_c", [P, S], U32)
-            z_s[name] = sb(name + "_s", [P, S], U8)
-            quantize(z_c[name], z_s[name], z_g[name], 0, S)
+        def z_quant(name, lo, hi):
+            if name not in z_c:
+                z_c[name] = sb(name + "_c", [P, S], U32)
+                z_s[name] = sb(name + "_s", [P, S], U8)
+            quantize(z_c[name], z_s[name], z_g[name], lo, hi)
 
-        for t in range(PACK):
+        w_deal("w3", w3_lo, 0, nc.scalar.copy)
+        for t in range(PACK - 1):
             y_fetch(t)
             y_mix(t)
         s_fetch(0)
-        w2_raw = load_weight("w2_raw", w2, 0, N, "raw1")
-        w_deal("w3", w3_raw, nc.vector.tensor_copy)
+        w3_hi = load_weight("w3_hi", w3, HALF, N, "mag0")
+        w_deal("w2", w2_lo, 0, nc.vector.tensor_copy)
+        y_fetch(3)
+        s_mix(0)
+        y_mix(3)
+        s_fetch(1)
+        s_put(0)
+        s_mix(1)
+        s_fetch(2)
+        w2_hi = load_weight("w2_hi", w2, HALF, N, "mag2")
+        s_put(1)
+        w_deal("w3", w3_hi, HALF // PACK, nc.scalar.copy)
+        s_mix(2)
         w_quant("w3")
-        for t in range(PACK - 1):
-            s_mix(t)
-            s_fetch(t + 1)
-            s_put(t)
-        y_put(0)
+        s_fetch(3)
+        s_put(2)
         s_mix(3)
-        y_put(1)
         s_put(3)
-        weave_first("z2", z2_all)
-        weave_one("z2", 3, st[3])
+        y_put(0)
+        y_put(1)
         y_put(2)
-        weave_first("z", z_all)
-        z_quant("z2")
-        h_bank = [psum.tile([P, S], F32, name="bankA%d" % t) for t in range(PACK)]
-        for t in range(PACK):
-            mx(h_bank[t], w_c["w3"], w_s["w3"], t, z_c["z2"], z_s["z2"], True, False)
+        w_deal("w2", w2_hi, HALF // PACK, nc.scalar.copy)
+        weave_first("z2", z2_all, nc.vector.tensor_copy)
+        weave_one("z2", 3, st[3], 0, S)
         y_put(3)
-        w_deal("w2", w2_raw, nc.scalar.copy)
-        weave_one("z", 2, yt[2])
-        weave_one("z", 3, yt[3])
+        nc.scalar.activation(warm[:, 1:2], yt[3][:, 0:1], ACT.Tanh)
+        z_quant("z2", 0, S)
         w_quant("w2")
-        z_quant("z")
-        for t in range(PACK):
-            mx(h_bank[t], w_c["w2"], w_s["w2"], t, z_c["z"], z_s["z"], False, True)
+        weave_first("z", z_all, nc.vector.tensor_copy)
+        for u in range(2):
+            weave_one("z", 3, yt[3], u * HALF, (u + 1) * HALF)
+        for u in range(2):
+            z_quant("z", u * HALF, (u + 1) * HALF)
+        h_bank = [psum.tile([P, S], F32, name="bankA%d" % t) for t in range(PACK)]
+        h0_hi = psum.tile([P, S], F32, name="bankB0")
+        for u, bank in enumerate((h_bank[0], h0_hi)):
+            mx(bank, w_c["w3"], w_s["w3"], 0, z_c["z2"], z_s["z2"], True, False, u * HALF, (u + 1) * HALF)
+            mx(bank, w_c["w2"], w_s["w2"], 0, z_c["z"], z_s["z"], False, True, u * HALF, (u + 1) * HALF)
+        for t in range(1, PACK):
+            mx(h_bank[t], w_c["w3"], w_s["w3"], t, z_c["z2"], z_s["z2"], True, False)
+            for u in range(2):
+                mx(h_bank[t], w_c["w2"], w_s["w2"], t, z_c["z"], z_s["z"], False, u == 1, u * HALF, (u + 1) * HALF)
 
         out_v = out.rearrange("(p t) n -> p t n", t=PACK)
         ht, pick, df, th = {}, {}, {}, {}
@@ -249,17 +270,35 @@ def tile_picked_jkeykdifknormfdif_none_p_kernel(
                 nc.vector.tensor_tensor(res[:], ht[t][:].indirect(offsets), th[t][:, cols], ALU.mult)
                 nc.sync.dma_start(out_v[:, t, cols], res[:])
 
-        h_window(0, nc.scalar.copy)
-        h_pick(0)
-        for t in range(1, PACK):
-            h_window(t, nc.vector.tensor_copy)
-        h_pick(1)
-        h_diff(0)
+        def h_twin(t):
+            pick[t] = sb("twin%d" % t, [P, S], F32)
+            nc.scalar.copy(pick[t][:], h_bank[t][:])
+
+        def h_diff_fused(t):
+            df[t] = sb("df%d" % t, [P, S], F32)
+            nc.vector.tensor_tensor(df[t][:], ht[t][:].indirect(l_n5[:]), pick[t][:], ALU.subtract)
+
+        ht[0] = sb("h0", [P, 2 * S], F32)
+        pick[0] = sb("twin0", [P, S], F32)
+        for u, (bank, copy) in enumerate(((h_bank[0], nc.scalar.copy), (h0_hi, nc.vector.tensor_copy))):
+            cols = slice(u * HALF, (u + 1) * HALF)
+            copy(ht[0][:, cols], bank[:, cols])
+            copy(pick[0][:, cols], bank[:, cols])
+        h_diff_fused(0)
+        h_window(1, nc.scalar.copy)
+        h_twin(1)
+        h_diff_fused(1)
+        h_window(2, nc.scalar.copy)
         h_tanh(0)
-        for t in range(1, PACK):
-            h_diff(t)
-            if t + 1 < PACK:
-                h_pick(t + 1)
-            h_out(t - 1, 1)
-            h_tanh(t)
+        h_twin(2)
+        h_out(0, 1)
+        h_diff_fused(2)
+        h_window(3, nc.scalar.copy)
+        h_tanh(1)
+        h_pick(3)
+        h_out(1, 1)
+        h_tanh(2)
+        h_diff(3)
+        h_out(2, 1)
+        h_tanh(3)
         h_out(PACK - 1, 2)

@@ -2,7 +2,7 @@ from contextlib import ExitStack
 
 import concourse.mybir as mybir
 
-K, T, S, N, H, G, W = 512, 1024, 512, 512, 512, 2048, 384
+T, S, N, H, G, W = 1024, 512, 512, 512, 2048, 384
 FLOPS = 4 * 2 * 512 * 512 * 512
 
 F32 = mybir.dt.float32
@@ -17,7 +17,9 @@ ACT = mybir.ActivationFunctionType
 
 P = 128
 PACK = 4
+LAST = PACK - 1
 HALF = 256
+GROUP = 16
 
 
 def tile_picked_jkeykdifknormfdif_none_p_kernel(
@@ -28,18 +30,46 @@ def tile_picked_jkeykdifknormfdif_none_p_kernel(
         keep = ctx.enter_context(tc.tile_pool(name="keep", bufs=1))
         psum = ctx.enter_context(tc.psum_pool(name="psum", bufs=1))
 
-        def sb(name, shape, dtype):
-            return keep.tile(shape, dtype, name=name, align_bytes=64)
+        def sb(name, shape, dtype, tag=None):
+            return keep.tile(shape, dtype, name=name, tag=tag or name, align_bytes=64)
 
         def load_list(name, src):
-            t = keep.tile([P, src.shape[1]], U16, name=name)
-            nc.sync.dma_start(t[:], src)
-            return t
+            offsets = keep.tile([P, src.shape[1]], U16, name=name)
+            nc.sync.dma_start(offsets[:], src)
+            return offsets
 
         def load_weight(name, w, lo, hi, tag):
-            raw = keep.tile([P, PACK, hi - lo], F32, name=name, tag=tag, align_bytes=64)
+            raw = sb(name, [P, PACK, hi - lo], F32, tag)
             nc.sync.dma_start(raw[:], w.rearrange("(p j) c -> p j c", j=PACK)[:, :, lo:hi])
             return raw
+
+        def gather_packed(name, table, offsets, dtype, tag=None):
+            picked = sb(name, [P, S], dtype, tag)
+            window = table[:].bitcast(U32) if dtype == U32 else table[:]
+            nc.vector.tensor_copy(picked[:], window.indirect(offsets[:]))
+            return picked
+
+        def quantize(codes, scales, woven, lo, hi):
+            nc.vector.quantize_mx(
+                out=codes[:, lo:hi].bitcast(FP8X4), scales=scales[:, lo:hi], in_=woven[:, PACK * lo : PACK * hi]
+            )
+
+        def deal_weight(woven, raw, lo, copy):
+            m0 = lo // PACK
+            dst = woven[:].rearrange("p (t m j) -> p m j t", t=PACK, j=PACK)[:, m0 : m0 + HALF // PACK, :, :]
+            copy(dst, raw[:].rearrange("p j (m t) -> p m j t", t=PACK))
+
+        def mx(bank, lhs, lhs_s, t, rhs, rhs_s, start, stop, lo=0, hi=S):
+            cols = slice(t * P, (t + 1) * P)
+            nc.tensor.matmul_mx(
+                out=bank[:, lo:hi],
+                lhsT=lhs[:, cols].bitcast(FP8X4),
+                lhsT_scale=lhs_s[:, cols],
+                rhs=rhs[:, lo:hi].bitcast(FP8X4),
+                rhs_scale=rhs_s[:, lo:hi],
+                start=start,
+                stop=stop,
+            )
 
         xs_tab = sb("xs_tab", [P, T], U8)
         ds_tab = sb("ds_tab", [P, G], U8)
@@ -56,7 +86,8 @@ def tile_picked_jkeykdifknormfdif_none_p_kernel(
         nc.sync.dma_start(xw_tab[:], x_words[0].rearrange("p n t -> p (n t)").bitcast(I32))
         l_two = load_list("l_two", two)
         for q in range(4):
-            nc.sync.dma_start(xs_tab[32 * q : 32 * q + 4, :].bitcast(I32), x_scales[0, 4 * q : 4 * q + 4, :].bitcast(I32))
+            rows = x_scales[0, 4 * q : 4 * q + 4, :]
+            nc.sync.dma_start(xs_tab[32 * q : 32 * q + 4, :].bitcast(I32), rows.bitcast(I32))
         nc.scalar.dma_start(ds_tab[0:P:8, :].bitcast(I32), d_scales[0].bitcast(I32))
         warm = sb("warm", [P, 2], F32)
         nc.scalar.activation(warm[:, 0:1], half[:], ACT.Abs_reciprocal_sqrt, bias=half[:])
@@ -73,32 +104,11 @@ def tile_picked_jkeykdifknormfdif_none_p_kernel(
         l_n4 = load_list("l_n4", n4)
         l_n3 = load_list("l_n3", n3)
 
-        def gather_packed(name, tab, lst, dtype, tag=None):
-            g = keep.tile([P, S], dtype, name=name, tag=tag or name, align_bytes=64)
-            src = tab[:].bitcast(U32) if dtype == U32 else tab[:]
-            nc.vector.tensor_copy(g[:], src.indirect(lst[:]))
-            return g
-
-        def quantize(codes, scales, grouped, lo, hi):
-            nc.vector.quantize_mx(out=codes[:, lo:hi].bitcast(FP8X4), scales=scales[:, lo:hi], in_=grouped[:, PACK * lo : PACK * hi])
-
-        def deal_views(grouped, raw, m0):
-            width = raw.shape[2] // PACK
-            dst = grouped[:].rearrange("p (t m j) -> p m j t", t=PACK, j=PACK)[:, m0 : m0 + width, :, :]
-            src = raw[:].rearrange("p j (m t) -> p m j t", t=PACK)
-            return dst, src
-
-        def mx(bank, lhs, lhs_s, t, rhs, rhs_s, start, stop, lo=0, hi=S):
-            cols = slice(t * P, (t + 1) * P)
-            nc.tensor.matmul_mx(out=bank[:, lo:hi], lhsT=lhs[:, cols].bitcast(FP8X4), lhsT_scale=lhs_s[:, cols],
-                                rhs=rhs[:, lo:hi].bitcast(FP8X4), rhs_scale=rhs_s[:, lo:hi], start=start, stop=stop)
-
         x1w = gather_packed("x1w", xw_tab, l_offs, U32)
         x1s = gather_packed("x1s", xs_tab, l_offs, U8)
         w1_g = sb("w1_g", [P, PACK * H], BF16)
         for u in range(2):
-            dst, src = deal_views(w1_g, w1_raw[u], u * HALF // PACK)
-            nc.scalar.copy(dst, src)
+            deal_weight(w1_g, w1_raw[u], u * HALF, nc.scalar.copy)
         l_n5 = load_list("l_n5", n5)
         l_n6 = load_list("l_n6", n6)
         w1_c = sb("w1_c", [P, H], U32)
@@ -110,24 +120,28 @@ def tile_picked_jkeykdifknormfdif_none_p_kernel(
 
         dsg = gather_packed("dsg", ds_tab, l_kidx, U8, "raw1")
         ds_deal = sb("ds_deal", [P, H], U8)
-        nc.vector.tensor_copy(ds_deal[:].rearrange("p (t m) -> p m t", t=PACK), dsg[:].rearrange("p (m t) -> p m t", t=PACK))
-        for u in range(4):
-            nc.sync.dma_start(ds_fin[u:P:32, :].bitcast(I32), ds_deal[8 * u : P : 32, :].bitcast(I32))
+        nc.vector.tensor_copy(
+            ds_deal[:].rearrange("p (t m) -> p m t", t=PACK), dsg[:].rearrange("p (m t) -> p m t", t=PACK)
+        )
+        for r in range(4):
+            nc.sync.dma_start(ds_fin[r:P:32, :].bitcast(I32), ds_deal[8 * r : P : 32, :].bitcast(I32))
         w2_lo = load_weight("w2_lo", w2, 0, HALF, "raw1")
         x2w = gather_packed("x2w", xw_tab, l_two, U32)
         x2s = gather_packed("x2s", xs_tab, l_two, U8)
         dwg = gather_packed("dwg", dw_tab, l_kidx, U32)
         dw_deal = sb("dw_deal", [P, H], U32)
-        nc.vector.tensor_copy(dw_deal[:].rearrange("p (t m) -> p t m", t=PACK), dwg[:].rearrange("p (m t) -> p t m", t=PACK))
+        nc.vector.tensor_copy(
+            dw_deal[:].rearrange("p (t m) -> p t m", t=PACK), dwg[:].rearrange("p (m t) -> p t m", t=PACK)
+        )
         s_bank = [psum.tile([P, S], F32, name="bankB%d" % t) for t in range(PACK)]
         for t in range(PACK):
             mx(s_bank[t], dw_deal, ds_fin, t, x2w, x2s, True, True)
         gk16 = sb("gk16", [P, PACK], F32)
         nc.gpsimd.tensor_scalar(gk16[:], gk_sb[:], 0.0625, 0.0, ALU.mult, ALU.add)
 
-        z_all = sb("z_all", [P, PACK - 1, S], F32)
-        z2_all = sb("z2_all", [P, PACK - 1, S], F32)
-        ra = keep.tile([P, PACK, W], F32, name="ra", tag="dw_tab", align_bytes=64)
+        z_all = sb("z_all", [P, LAST, S], F32)
+        z2_all = sb("z2_all", [P, LAST, S], F32)
+        ra = sb("ra", [P, PACK, W], F32, "dw_tab")
         yt, st, pa, rs, rb = {}, {}, {}, {}, {}
 
         def y_fetch(t):
@@ -141,7 +155,7 @@ def tile_picked_jkeykdifknormfdif_none_p_kernel(
 
         def y_put(t):
             nc.scalar.activation(yt[t][:].indirect(l_n1[:]), ra[:, t, :], ACT.Copy)
-            if t < PACK - 1:
+            if t < LAST:
                 nc.sync.dma_start(z_all[:, t, :], yt[t][:, 0:S])
 
         def s_fetch(t):
@@ -160,145 +174,135 @@ def tile_picked_jkeykdifknormfdif_none_p_kernel(
 
         def s_put(t):
             nc.vector.tensor_tensor(st[t][:].indirect(l_n3[:]), rb[t][:], rs[t][:], ALU.mult)
-            if t < PACK - 1:
+            if t < LAST:
                 nc.sync.dma_start(z2_all[:, t, :], st[t][:])
 
-        w_g = {}
-        w_c = {}
-        w_s = {}
+        def weave_first(name, planes):
+            woven = sb(name, [P, PACK * S], BF16, "rs%d" % LAST)
+            view = woven[:].rearrange("p (c i t) -> p c t i", i=4, t=PACK)
+            nc.vector.tensor_copy(view[:, :, 0:LAST, :], planes[:].rearrange("p t (c i) -> p c t i", i=4))
+            return woven
 
-        def w_deal(name, raw, m0, copy):
-            if name not in w_g:
-                w_g[name] = sb(name + "_g", [P, PACK * N], BF16)
-            dst, src = deal_views(w_g[name], raw, m0)
-            copy(dst, src)
+        def weave_last(woven, plane, lo, hi):
+            nc.vector.tensor_copy(woven[:].rearrange("p (c t) -> p c t", t=PACK)[:, lo:hi, LAST], plane[:, lo:hi])
 
-        def w_quant(name):
-            w_c[name] = sb(name + "_c", [P, N], U32)
-            w_s[name] = sb(name + "_s", [P, N], U8)
-            quantize(w_c[name], w_s[name], w_g[name], 0, N)
+        def mx_tiles(name, width):
+            return sb(name + "_c", [P, width], U32), sb(name + "_s", [P, width], U8)
 
-        z_g, z_c, z_s = {}, {}, {}
-
-        def weave_first(name, planes, copy):
-            z_g[name] = keep.tile([P, PACK * S], BF16, name=name + "_g", tag="rs3", align_bytes=64)
-            view = z_g[name][:].rearrange("p (c i t) -> p c t i", i=4, t=PACK)
-            copy(view[:, :, 0 : planes.shape[1], :], planes[:].rearrange("p t (c i) -> p c t i", i=4))
-
-        def weave_one(name, t, plane, lo, hi):
-            nc.vector.tensor_copy(z_g[name][:].rearrange("p (c t) -> p c t", t=PACK)[:, lo:hi, t], plane[:, lo:hi])
-
-        def z_quant(name, lo, hi):
-            if name not in z_c:
-                z_c[name] = sb(name + "_c", [P, S], U32)
-                z_s[name] = sb(name + "_s", [P, S], U8)
-            quantize(z_c[name], z_s[name], z_g[name], lo, hi)
-
-        w_deal("w3", w3_lo, 0, nc.scalar.copy)
-        for t in range(PACK - 1):
+        w3_g = sb("w3_g", [P, PACK * N], BF16)
+        deal_weight(w3_g, w3_lo, 0, nc.scalar.copy)
+        for t in range(LAST):
             y_fetch(t)
             y_mix(t)
         s_fetch(0)
         w3_hi = load_weight("w3_hi", w3, HALF, N, "mag0")
-        w_deal("w2", w2_lo, 0, nc.vector.tensor_copy)
-        y_fetch(3)
+        w2_g = sb("w2_g", [P, PACK * N], BF16)
+        deal_weight(w2_g, w2_lo, 0, nc.vector.tensor_copy)
+        y_fetch(LAST)
         s_mix(0)
-        y_mix(3)
+        y_mix(LAST)
         s_fetch(1)
         s_put(0)
         s_mix(1)
         s_fetch(2)
         w2_hi = load_weight("w2_hi", w2, HALF, N, "mag2")
         s_put(1)
-        w_deal("w3", w3_hi, HALF // PACK, nc.scalar.copy)
+        deal_weight(w3_g, w3_hi, HALF, nc.scalar.copy)
         s_mix(2)
-        w_quant("w3")
-        s_fetch(3)
+        w3_c, w3_s = mx_tiles("w3", N)
+        quantize(w3_c, w3_s, w3_g, 0, N)
+        s_fetch(LAST)
         s_put(2)
-        s_mix(3)
-        s_put(3)
-        y_put(0)
-        y_put(1)
-        y_put(2)
-        w_deal("w2", w2_hi, HALF // PACK, nc.scalar.copy)
-        weave_first("z2", z2_all, nc.vector.tensor_copy)
-        weave_one("z2", 3, st[3], 0, S)
-        y_put(3)
-        nc.scalar.activation(warm[:, 1:2], yt[3][:, 0:1], ACT.Tanh)
-        z_quant("z2", 0, S)
-        w_quant("w2")
-        weave_first("z", z_all, nc.vector.tensor_copy)
+        s_mix(LAST)
+        s_put(LAST)
+        for t in range(LAST):
+            y_put(t)
+        deal_weight(w2_g, w2_hi, HALF, nc.scalar.copy)
+        z2_g = weave_first("z2_g", z2_all)
+        weave_last(z2_g, st[LAST], 0, S)
+        y_put(LAST)
+        nc.scalar.activation(warm[:, 1:2], yt[LAST][:, 0:1], ACT.Tanh)
+        z2_c, z2_s = mx_tiles("z2", S)
+        quantize(z2_c, z2_s, z2_g, 0, S)
+        w2_c, w2_s = mx_tiles("w2", N)
+        quantize(w2_c, w2_s, w2_g, 0, N)
+        z_g = weave_first("z_g", z_all)
         for u in range(2):
-            weave_one("z", 3, yt[3], u * HALF, (u + 1) * HALF)
+            weave_last(z_g, yt[LAST], u * HALF, (u + 1) * HALF)
+        z_c, z_s = mx_tiles("z", S)
         for u in range(2):
-            z_quant("z", u * HALF, (u + 1) * HALF)
+            quantize(z_c, z_s, z_g, u * HALF, (u + 1) * HALF)
+
         h_bank = [psum.tile([P, S], F32, name="bankA%d" % t) for t in range(PACK)]
         h0_hi = psum.tile([P, S], F32, name="bankB0")
         for u, bank in enumerate((h_bank[0], h0_hi)):
-            mx(bank, w_c["w3"], w_s["w3"], 0, z_c["z2"], z_s["z2"], True, False, u * HALF, (u + 1) * HALF)
-            mx(bank, w_c["w2"], w_s["w2"], 0, z_c["z"], z_s["z"], False, True, u * HALF, (u + 1) * HALF)
+            mx(bank, w3_c, w3_s, 0, z2_c, z2_s, True, False, u * HALF, (u + 1) * HALF)
+            mx(bank, w2_c, w2_s, 0, z_c, z_s, False, True, u * HALF, (u + 1) * HALF)
         for t in range(1, PACK):
-            mx(h_bank[t], w_c["w3"], w_s["w3"], t, z_c["z2"], z_s["z2"], True, False)
+            mx(h_bank[t], w3_c, w3_s, t, z2_c, z2_s, True, False)
             for u in range(2):
-                mx(h_bank[t], w_c["w2"], w_s["w2"], t, z_c["z"], z_s["z"], False, u == 1, u * HALF, (u + 1) * HALF)
+                mx(h_bank[t], w2_c, w2_s, t, z_c, z_s, False, u == 1, u * HALF, (u + 1) * HALF)
 
         out_v = out.rearrange("(p t) n -> p t n", t=PACK)
-        ht, pick, df, th = {}, {}, {}, {}
+        ht, twin, df, th = {}, {}, {}, {}
 
-        def h_window(t, copy):
+        def h_window(t):
             ht[t] = sb("h%d" % t, [P, 2 * S], F32)
-            copy(ht[t][:, 0:S], h_bank[t][:])
+            nc.scalar.copy(ht[t][:, 0:S], h_bank[t][:])
 
-        def h_pick(t):
-            pick[t] = sb("pick%d" % t, [P, S], F32)
-            nc.scalar.activation(pick[t][:], ht[t][:].indirect(l_n5[:]), ACT.Copy)
+        def h_twin(t):
+            twin[t] = sb("twin%d" % t, [P, S], F32)
+            nc.scalar.copy(twin[t][:], h_bank[t][:])
 
-        def h_diff(t):
+        def h_diff(t, pieces):
             df[t] = sb("df%d" % t, [P, S], F32)
-            nc.vector.tensor_tensor(df[t][:], pick[t][:], h_bank[t][:], ALU.subtract)
+            width = S // pieces
+            for u in range(pieces):
+                cols = slice(u * width, (u + 1) * width)
+                offsets = l_n5[:, u * width // GROUP : (u + 1) * width // GROUP]
+                nc.vector.tensor_tensor(df[t][:, cols], ht[t][:].indirect(offsets), twin[t][:, cols], ALU.subtract)
 
         def h_tanh(t):
             th[t] = sb("th%d" % t, [P, S], F32)
             nc.scalar.activation(th[t][:], df[t][:], ACT.Tanh)
 
-        def h_out(t, pieces):
-            width = S // pieces
-            for u in range(pieces):
-                res = sb("res%d_%d" % (t, u), [P, width], F32)
-                cols = slice(u * width, (u + 1) * width)
-                offsets = l_n6[:, u * width // 16 : (u + 1) * width // 16]
-                nc.vector.tensor_tensor(res[:], ht[t][:].indirect(offsets), th[t][:, cols], ALU.mult)
-                nc.sync.dma_start(out_v[:, t, cols], res[:])
+        def h_out(t):
+            res = sb("res%d" % t, [P, S], F32)
+            nc.vector.tensor_tensor(res[:], ht[t][:].indirect(l_n6[:]), th[t][:], ALU.mult)
+            nc.sync.dma_start(out_v[:, t, :], res[:])
 
-        def h_twin(t):
-            pick[t] = sb("twin%d" % t, [P, S], F32)
-            nc.scalar.copy(pick[t][:], h_bank[t][:])
-
-        def h_diff_fused(t):
-            df[t] = sb("df%d" % t, [P, S], F32)
-            nc.vector.tensor_tensor(df[t][:], ht[t][:].indirect(l_n5[:]), pick[t][:], ALU.subtract)
+        def h_pick(name, offsets):
+            picked = sb(name, [P, S], F32)
+            nc.scalar.activation(picked[:], ht[LAST][:].indirect(offsets[:]), ACT.Copy)
+            return picked
 
         ht[0] = sb("h0", [P, 2 * S], F32)
-        pick[0] = sb("twin0", [P, S], F32)
-        for u, (bank, copy) in enumerate(((h_bank[0], nc.scalar.copy), (h0_hi, nc.vector.tensor_copy))):
+        twin[0] = sb("twin0", [P, S], F32)
+        for u, (bank, copy) in enumerate(((h_bank[0], nc.vector.tensor_copy), (h0_hi, nc.scalar.copy))):
             cols = slice(u * HALF, (u + 1) * HALF)
             copy(ht[0][:, cols], bank[:, cols])
-            copy(pick[0][:, cols], bank[:, cols])
-        h_diff_fused(0)
-        h_window(1, nc.scalar.copy)
+            copy(twin[0][:, cols], bank[:, cols])
+        h_diff(0, 2)
+        h_window(1)
         h_twin(1)
-        h_diff_fused(1)
-        h_window(2, nc.scalar.copy)
+        h_diff(1, 1)
+        h_window(2)
         h_tanh(0)
         h_twin(2)
-        h_out(0, 1)
-        h_diff_fused(2)
-        h_window(3, nc.scalar.copy)
+        h_out(0)
+        h_diff(2, 1)
+        h_window(LAST)
         h_tanh(1)
-        h_pick(3)
-        h_out(1, 1)
+        picked5 = h_pick("picked5", l_n5)
+        h_out(1)
         h_tanh(2)
-        h_diff(3)
-        h_out(2, 1)
-        h_tanh(3)
-        h_out(PACK - 1, 2)
+        df[LAST] = sb("df3", [P, S], F32)
+        nc.vector.tensor_tensor(df[LAST][:], picked5[:], h_bank[LAST][:], ALU.subtract)
+        picked6 = h_pick("picked6", l_n6)
+        h_out(2)
+        h_tanh(LAST)
+        for u in range(2):
+            cols = slice(u * HALF, (u + 1) * HALF)
+            res = sb("res3_%d" % u, [P, HALF], F32)
+            nc.vector.tensor_tensor(res[:], picked6[:, cols], th[LAST][:, cols], ALU.mult)
+            nc.sync.dma_start(out_v[:, LAST, cols], res[:])

from contextlib import ExitStack

import concourse.mybir as mybir

T, S, N, H, G, W = 1024, 512, 512, 512, 2048, 384
FLOPS = 4 * 2 * 512 * 512 * 512

F32 = mybir.dt.float32
BF16 = mybir.dt.bfloat16
I32 = mybir.dt.int32
U32 = mybir.dt.uint32
U16 = mybir.dt.uint16
U8 = mybir.dt.uint8
FP8X4 = mybir.dt.float8_e4m3fn_x4
ALU = mybir.AluOpType
ACT = mybir.ActivationFunctionType

P = 128
PACK = 4
LAST = PACK - 1
HALF = 256
GROUP = 16


def tile_picked_jkeykdifknormfdif_none_p_kernel(
    tc, x_words, x_scales, w1, d_words, d_scales, gn, gk, w2, w3, offs, kidx, two, n1, n2, n3, n4, n5, n6, out
):
    nc = tc.nc
    with ExitStack() as ctx:
        keep = ctx.enter_context(tc.tile_pool(name="keep", bufs=1))
        psum = ctx.enter_context(tc.psum_pool(name="psum", bufs=1))

        def sb(name, shape, dtype, tag=None):
            return keep.tile(shape, dtype, name=name, tag=tag or name, align_bytes=64)

        def load_list(name, src):
            offsets = keep.tile([P, src.shape[1]], U16, name=name)
            nc.sync.dma_start(offsets[:], src)
            return offsets

        def load_weight(name, w, lo, hi, tag):
            raw = sb(name, [P, PACK, hi - lo], F32, tag)
            nc.sync.dma_start(raw[:], w.rearrange("(p j) c -> p j c", j=PACK)[:, :, lo:hi])
            return raw

        def gather_packed(name, table, offsets, dtype, tag=None):
            picked = sb(name, [P, S], dtype, tag)
            window = table[:].bitcast(U32) if dtype == U32 else table[:]
            nc.vector.tensor_copy(picked[:], window.indirect(offsets[:]))
            return picked

        def quantize(codes, scales, woven, lo, hi):
            nc.vector.quantize_mx(
                out=codes[:, lo:hi].bitcast(FP8X4), scales=scales[:, lo:hi], in_=woven[:, PACK * lo : PACK * hi]
            )

        def deal_weight(woven, raw, lo, copy):
            m0 = lo // PACK
            dst = woven[:].rearrange("p (t m j) -> p m j t", t=PACK, j=PACK)[:, m0 : m0 + HALF // PACK, :, :]
            copy(dst, raw[:].rearrange("p j (m t) -> p m j t", t=PACK))

        def mx(bank, lhs, lhs_s, t, rhs, rhs_s, start, stop, lo=0, hi=S):
            cols = slice(t * P, (t + 1) * P)
            nc.tensor.matmul_mx(
                out=bank[:, lo:hi],
                lhsT=lhs[:, cols].bitcast(FP8X4),
                lhsT_scale=lhs_s[:, cols],
                rhs=rhs[:, lo:hi].bitcast(FP8X4),
                rhs_scale=rhs_s[:, lo:hi],
                start=start,
                stop=stop,
            )

        xs_tab = sb("xs_tab", [P, T], U8)
        ds_tab = sb("ds_tab", [P, G], U8)
        ds_fin = sb("ds_fin", [P, H], U8)
        half = sb("half", [P, 1], F32)
        nc.gpsimd.memset(xs_tab[:].bitcast(I32), 0)
        nc.gpsimd.memset(ds_tab[:].bitcast(I32), 0)
        nc.gpsimd.memset(half[:], 0.5)
        nc.gpsimd.memset(ds_fin[:].bitcast(I32), 0)

        l_offs = load_list("l_offs", offs)
        l_kidx = load_list("l_kidx", kidx)
        xw_tab = sb("xw_tab", [P, T], I32)
        nc.sync.dma_start(xw_tab[:], x_words[0].rearrange("p n t -> p (n t)").bitcast(I32))
        l_two = load_list("l_two", two)
        for q in range(4):
            rows = x_scales[0, 4 * q : 4 * q + 4, :]
            nc.sync.dma_start(xs_tab[32 * q : 32 * q + 4, :].bitcast(I32), rows.bitcast(I32))
        nc.scalar.dma_start(ds_tab[0:P:8, :].bitcast(I32), d_scales[0].bitcast(I32))
        warm = sb("warm", [P, 2], F32)
        nc.scalar.activation(warm[:, 0:1], half[:], ACT.Abs_reciprocal_sqrt, bias=half[:])
        w1_raw = [load_weight("w1_raw%d" % u, w1, u * HALF, (u + 1) * HALF, "raw%d" % u) for u in range(2)]
        w3_lo = load_weight("w3_lo", w3, 0, HALF, "w3_lo")
        l_n2 = load_list("l_n2", n2)
        l_n1 = load_list("l_n1", n1)
        dw_tab = sb("dw_tab", [P, G], I32)
        nc.sync.dma_start(dw_tab[:], d_words[0].rearrange("p n t -> p (n t)").bitcast(I32))
        gn_sb = sb("gn_sb", [P, PACK], F32)
        gk_sb = sb("gk_sb", [P, PACK], F32)
        nc.gpsimd.dma_start(gn_sb[:], gn.rearrange("(p t) o -> p (t o)", t=PACK))
        nc.gpsimd.dma_start(gk_sb[:], gk.rearrange("(p t) o -> p (t o)", t=PACK))
        l_n4 = load_list("l_n4", n4)
        l_n3 = load_list("l_n3", n3)

        x1w = gather_packed("x1w", xw_tab, l_offs, U32)
        x1s = gather_packed("x1s", xs_tab, l_offs, U8)
        w1_g = sb("w1_g", [P, PACK * H], BF16)
        for u in range(2):
            deal_weight(w1_g, w1_raw[u], u * HALF, nc.scalar.copy)
        l_n5 = load_list("l_n5", n5)
        l_n6 = load_list("l_n6", n6)
        w1_c = sb("w1_c", [P, H], U32)
        w1_s = sb("w1_s", [P, H], U8)
        y_bank = [psum.tile([P, S], F32, name="bankA%d" % t) for t in range(PACK)]
        for t in range(PACK):
            quantize(w1_c, w1_s, w1_g, t * P, (t + 1) * P)
            mx(y_bank[t], w1_c, w1_s, t, x1w, x1s, True, True)

        dsg = gather_packed("dsg", ds_tab, l_kidx, U8, "raw1")
        ds_deal = sb("ds_deal", [P, H], U8)
        nc.vector.tensor_copy(
            ds_deal[:].rearrange("p (t m) -> p m t", t=PACK), dsg[:].rearrange("p (m t) -> p m t", t=PACK)
        )
        for r in range(4):
            nc.sync.dma_start(ds_fin[r:P:32, :].bitcast(I32), ds_deal[8 * r : P : 32, :].bitcast(I32))
        w2_lo = load_weight("w2_lo", w2, 0, HALF, "raw1")
        x2w = gather_packed("x2w", xw_tab, l_two, U32)
        x2s = gather_packed("x2s", xs_tab, l_two, U8)
        dwg = gather_packed("dwg", dw_tab, l_kidx, U32)
        dw_deal = sb("dw_deal", [P, H], U32)
        nc.vector.tensor_copy(
            dw_deal[:].rearrange("p (t m) -> p t m", t=PACK), dwg[:].rearrange("p (m t) -> p t m", t=PACK)
        )
        s_bank = [psum.tile([P, S], F32, name="bankB%d" % t) for t in range(PACK)]
        for t in range(PACK):
            mx(s_bank[t], dw_deal, ds_fin, t, x2w, x2s, True, True)
        gk16 = sb("gk16", [P, PACK], F32)
        nc.gpsimd.tensor_scalar(gk16[:], gk_sb[:], 0.0625, 0.0, ALU.mult, ALU.add)

        z_all = sb("z_all", [P, LAST, S], F32)
        z2_all = sb("z2_all", [P, LAST, S], F32)
        ra = sb("ra", [P, PACK, W], F32, "dw_tab")
        yt, st, pa, rs, rb = {}, {}, {}, {}, {}

        def y_fetch(t):
            yt[t] = sb("y%d" % t, [P, S + W], F32)
            nc.scalar.activation(yt[t][:, 0:S], y_bank[t][:], ACT.Copy, scale=gn_sb[:, t : t + 1])
            pa[t] = sb("pa%d" % t, [P, W], F32)
            nc.scalar.activation(pa[t][:], yt[t][:].indirect(l_n2[:]), ACT.Copy, scale=-0.5)

        def y_mix(t):
            nc.vector.tensor_tensor(ra[:, t, :], yt[t][:].indirect(l_n1[:]), pa[t][:], ALU.add)

        def y_put(t):
            nc.scalar.activation(yt[t][:].indirect(l_n1[:]), ra[:, t, :], ACT.Copy)
            if t < LAST:
                nc.sync.dma_start(z_all[:, t, :], yt[t][:, 0:S])

        def s_fetch(t):
            mag = sb("mag%d" % t, [P, S], F32)
            nc.scalar.activation(mag[:], s_bank[t][:], ACT.Abs, scale=0.0625)
            den = yt[t][:, S : S + W]
            nc.scalar.activation(den, mag[:].indirect(l_n4[:]), ACT.Copy)
            st[t] = sb("s%d" % t, [P, S], F32)
            nc.scalar.activation(st[t][:], s_bank[t][:], ACT.Copy, scale=gk16[:, t : t + 1])
            rs[t] = sb("rs%d" % t, [P, W], F32)
            nc.scalar.activation(rs[t][:], den, ACT.Abs_reciprocal_sqrt, bias=half[:])

        def s_mix(t):
            rb[t] = sb("rb%d" % t, [P, W], F32)
            nc.vector.tensor_tensor(rb[t][:], st[t][:].indirect(l_n3[:]), rs[t][:], ALU.mult)

        def s_put(t):
            nc.vector.tensor_tensor(st[t][:].indirect(l_n3[:]), rb[t][:], rs[t][:], ALU.mult)
            if t < LAST:
                nc.sync.dma_start(z2_all[:, t, :], st[t][:])

        def weave_first(name, planes):
            woven = sb(name, [P, PACK * S], BF16, "rs%d" % LAST)
            view = woven[:].rearrange("p (c i t) -> p c t i", i=4, t=PACK)
            nc.vector.tensor_copy(view[:, :, 0:LAST, :], planes[:].rearrange("p t (c i) -> p c t i", i=4))
            return woven

        def weave_last(woven, plane, lo, hi):
            nc.vector.tensor_copy(woven[:].rearrange("p (c t) -> p c t", t=PACK)[:, lo:hi, LAST], plane[:, lo:hi])

        def mx_tiles(name, width):
            return sb(name + "_c", [P, width], U32), sb(name + "_s", [P, width], U8)

        w3_g = sb("w3_g", [P, PACK * N], BF16)
        deal_weight(w3_g, w3_lo, 0, nc.scalar.copy)
        for t in range(LAST):
            y_fetch(t)
            y_mix(t)
        s_fetch(0)
        w3_hi = load_weight("w3_hi", w3, HALF, N, "mag0")
        w2_g = sb("w2_g", [P, PACK * N], BF16)
        deal_weight(w2_g, w2_lo, 0, nc.vector.tensor_copy)
        y_fetch(LAST)
        s_mix(0)
        y_mix(LAST)
        s_fetch(1)
        s_put(0)
        s_mix(1)
        s_fetch(2)
        w2_hi = load_weight("w2_hi", w2, HALF, N, "mag2")
        s_put(1)
        deal_weight(w3_g, w3_hi, HALF, nc.scalar.copy)
        s_mix(2)
        w3_c, w3_s = mx_tiles("w3", N)
        quantize(w3_c, w3_s, w3_g, 0, N)
        s_fetch(LAST)
        s_put(2)
        s_mix(LAST)
        s_put(LAST)
        for t in range(LAST):
            y_put(t)
        deal_weight(w2_g, w2_hi, HALF, nc.scalar.copy)
        z2_g = weave_first("z2_g", z2_all)
        weave_last(z2_g, st[LAST], 0, S)
        y_put(LAST)
        nc.scalar.activation(warm[:, 1:2], yt[LAST][:, 0:1], ACT.Tanh)
        z2_c, z2_s = mx_tiles("z2", S)
        quantize(z2_c, z2_s, z2_g, 0, S)
        w2_c, w2_s = mx_tiles("w2", N)
        quantize(w2_c, w2_s, w2_g, 0, N)
        z_g = weave_first("z_g", z_all)
        for u in range(2):
            weave_last(z_g, yt[LAST], u * HALF, (u + 1) * HALF)
        z_c, z_s = mx_tiles("z", S)
        for u in range(2):
            quantize(z_c, z_s, z_g, u * HALF, (u + 1) * HALF)

        h_bank = [psum.tile([P, S], F32, name="bankA%d" % t) for t in range(PACK)]
        h0_hi = psum.tile([P, S], F32, name="bankB0")
        for u, bank in enumerate((h_bank[0], h0_hi)):
            mx(bank, w3_c, w3_s, 0, z2_c, z2_s, True, False, u * HALF, (u + 1) * HALF)
            mx(bank, w2_c, w2_s, 0, z_c, z_s, False, True, u * HALF, (u + 1) * HALF)
        for t in range(1, PACK):
            mx(h_bank[t], w3_c, w3_s, t, z2_c, z2_s, True, False)
            for u in range(2):
                mx(h_bank[t], w2_c, w2_s, t, z_c, z_s, False, u == 1, u * HALF, (u + 1) * HALF)

        out_v = out.rearrange("(p t) n -> p t n", t=PACK)
        ht, twin, df, th = {}, {}, {}, {}

        def h_window(t):
            ht[t] = sb("h%d" % t, [P, 2 * S], F32)
            nc.scalar.copy(ht[t][:, 0:S], h_bank[t][:])

        def h_twin(t):
            twin[t] = sb("twin%d" % t, [P, S], F32)
            nc.scalar.copy(twin[t][:], h_bank[t][:])

        def h_diff(t, pieces):
            df[t] = sb("df%d" % t, [P, S], F32)
            width = S // pieces
            for u in range(pieces):
                cols = slice(u * width, (u + 1) * width)
                offsets = l_n5[:, u * width // GROUP : (u + 1) * width // GROUP]
                nc.vector.tensor_tensor(df[t][:, cols], ht[t][:].indirect(offsets), twin[t][:, cols], ALU.subtract)

        def h_tanh(t):
            th[t] = sb("th%d" % t, [P, S], F32)
            nc.scalar.activation(th[t][:], df[t][:], ACT.Tanh)

        def h_out(t):
            res = sb("res%d" % t, [P, S], F32)
            nc.vector.tensor_tensor(res[:], ht[t][:].indirect(l_n6[:]), th[t][:], ALU.mult)
            nc.sync.dma_start(out_v[:, t, :], res[:])

        def h_pick(name, offsets):
            picked = sb(name, [P, S], F32)
            nc.scalar.activation(picked[:], ht[LAST][:].indirect(offsets[:]), ACT.Copy)
            return picked

        ht[0] = sb("h0", [P, 2 * S], F32)
        twin[0] = sb("twin0", [P, S], F32)
        for u, (bank, copy) in enumerate(((h_bank[0], nc.vector.tensor_copy), (h0_hi, nc.scalar.copy))):
            cols = slice(u * HALF, (u + 1) * HALF)
            copy(ht[0][:, cols], bank[:, cols])
            copy(twin[0][:, cols], bank[:, cols])
        h_diff(0, 2)
        h_window(1)
        h_twin(1)
        h_diff(1, 1)
        h_window(2)
        h_tanh(0)
        h_twin(2)
        h_out(0)
        h_diff(2, 1)
        h_window(LAST)
        h_tanh(1)
        picked5 = h_pick("picked5", l_n5)
        h_out(1)
        h_tanh(2)
        df[LAST] = sb("df3", [P, S], F32)
        nc.vector.tensor_tensor(df[LAST][:], picked5[:], h_bank[LAST][:], ALU.subtract)
        picked6 = h_pick("picked6", l_n6)
        h_out(2)
        h_tanh(LAST)
        for u in range(2):
            cols = slice(u * HALF, (u + 1) * HALF)
            res = sb("res3_%d" % u, [P, HALF], F32)
            nc.vector.tensor_tensor(res[:], picked6[:, cols], th[LAST][:, cols], ALU.mult)
            nc.sync.dma_start(out_v[:, LAST, cols], res[:])
